import numpy as np
import ml_dtypes


def mxq(x, axis, fmt="e4m3"):
    dtype, down = {"e4m3": (ml_dtypes.float8_e4m3fn, 7), "e5m2": (ml_dtypes.float8_e5m2, 14)}[fmt]
    v = np.moveaxis(np.asarray(x, np.float32).astype(ml_dtypes.bfloat16).astype(np.float64), axis, -1)
    blocks = v.reshape(v.shape[:-1] + (-1, 32))
    amax = np.abs(blocks).max(-1, keepdims=True)
    byte = np.maximum(np.where(amax > 0, np.frexp(amax)[1] - 1 + 127, 0) - down, 1)
    scale = np.exp2(byte - 127.0)
    codes = (blocks / scale).astype(np.float32).astype(dtype).astype(np.float64)
    return np.moveaxis((codes * scale).reshape(v.shape), -1, axis)


WIDE = False


def mx_kscale(k):
    if not WIDE:
        return np.ones(k)
    levels = np.array([10, -10, 5, -5, 0])
    if k % 512:
        return np.exp2(np.random.permutation(np.resize(levels, k // 32))).repeat(32)
    a = np.empty((k // 512, 16))
    for p in range(k // 512):
        a[p, :8] = np.random.permutation(np.resize(levels, 8))
        for g in range(8):
            far = levels[np.abs(levels - a[p, g]) >= 10]
            a[p, g + 8] = far[np.random.randint(len(far))]
    return np.exp2(a.ravel()).repeat(32)


def f64(x):
    return np.asarray(x).astype(np.float64)


def striped(idx):
    return np.tile(idx.reshape(-1, 16).T, (8, 1)).astype(np.uint16)


def unstriped(offs):
    return offs[:16].T.reshape(-1).astype(np.int64)


E2M1 = np.array([0.0, 0.5, 1.0, 1.5, 2.0, 3.0, 4.0, 6.0, -0.0, -0.5, -1.0, -1.5, -2.0, -3.0, -4.0, -6.0])


def pack_weight(w, fmt):
    k, n = w.shape
    w = f64(np.asarray(w, np.float32).astype(ml_dtypes.bfloat16)).reshape(k // 32, 32, n)
    amax = np.abs(w).max(1)
    if fmt == "e4m3":
        byte = np.frexp(amax)[1] - 1 + 127 - 7
    else:
        mant, ex = np.frexp(amax / 6.0)
        byte = np.where(mant > 0.5, ex, ex - 1) + 127
    byte = np.clip(np.where(amax > 0, byte, 1), 1, 254)
    scaled = (w * np.exp2(127.0 - byte)[:, None, :]).reshape(k, n).astype(np.float32)
    by_word = np.ascontiguousarray(scaled.reshape(k // 512, 128, 4, n).transpose(0, 1, 3, 2))
    if fmt == "e4m3":
        words = by_word.astype(ml_dtypes.float8_e4m3fn).view(np.uint8)
    else:
        c = by_word.astype(ml_dtypes.float4_e2m1fn).view(np.uint8) & 0xF
        words = (c[..., 0::2] | (c[..., 1::2] << 4)).reshape(k // 512, 128, 2 * n)
    return np.ascontiguousarray(words), np.ascontiguousarray(byte.astype(np.uint8).reshape(k // 512, 16, n))


def unpack_weight(words, scales, fmt):
    g, _, n = scales.shape
    words = np.ascontiguousarray(words).reshape(g, 128, n, -1)
    if fmt == "e4m3":
        vals = words.view(ml_dtypes.float8_e4m3fn).astype(np.float64)
    else:
        nib = np.empty((g, 128, n, 4), np.uint8)
        nib[..., 0::2] = words & 0xF
        nib[..., 1::2] = words >> 4
        vals = E2M1[nib]
    vals = vals * np.repeat(np.exp2(scales.astype(np.float64) - 127.0), 8, axis=1)[..., None]
    return vals.transpose(0, 1, 3, 2).reshape(g * 512, n)


def gelu(v):
    return 0.5 * v * (1.0 + np.tanh(np.sqrt(2.0 / np.pi) * (v + 0.044715 * v**3)))


K, T, S, H, N, P, T2, B = 1024, 4096, 1024, 1024, 512, 1024, 2048, 128

def setup_inputs():
    n = np.random.standard_normal
    s = mx_kscale(K)[:, None]
    u = mx_kscale(H)[:, None]
    d = {}
    d["tab_words"], d["tab_scales"] = pack_weight(n((K, T)) * s, "e4m3")
    d["offs"] = striped(np.random.permutation(T)[:S])
    d["w1"] = (n((K, H)) * 0.5 / K ** 0.5 / s).astype(np.float32)
    d["gain"] = (2.5 * np.exp(0.2 * n(H)) * u[:, 0]).astype(np.float32)
    d["page0"] = (n((H, T2)) * u).astype(np.float32)
    d["offs2"] = striped(np.random.permutation(T2)[:S])
    d["wgs"] = np.exp(0.3 * n((B, S))).astype(np.float32)
    d["offs3"] = striped(np.random.permutation(T2)[:P])
    d["steep"] = (2.0 * np.exp(0.2 * n(H)) / u[:, 0]).astype(np.float32)
    d["lift"] = (np.exp(0.3 * n(H)) * u[:, 0]).astype(np.float32)
    d["w2"] = (n((H, N)) / H ** 0.5 / u).astype(np.float32)
    d["w3_words"], d["w3_scales"] = pack_weight(n((H, N)) * 2.5 / H ** 0.5 / u, "e2m1")
    d["page1"] = n((N, T2)).astype(np.float32)
    d["offs4"] = striped(np.random.permutation(T2)[:P])
    d["wgo"] = np.exp(0.3 * n((B, P))).astype(np.float32)
    return d

def reference(tab_words, tab_scales, offs, w1, gain, page0, offs2, wgs, offs3, steep, lift, w2, w3_words, w3_scales, page1, offs4, wgo):
    v = unpack_weight(tab_words, tab_scales, "e4m3")[:, unstriped(offs)]
    b = mxq(f64(w1), 0, "e4m3").T @ v
    h = f64(gain)[:, None] * (b * np.cos(b))
    page = f64(page0).copy()
    page[:, unstriped(offs2)] = np.tile(f64(wgs), (H // B, 1)) * h
    x = page[:, unstriped(offs3)]
    f = f64(lift)[:, None] * (1.0 / (1.0 + np.exp(-(f64(steep)[:, None] * x))))
    y1 = mxq(f64(w2), 0, "e4m3").T @ mxq(x, 0, "e4m3")
    y2 = unpack_weight(w3_words, w3_scales, "e2m1").T @ mxq(f, 0, "e4m3")
    y = y1 - y2
    out = f64(page1).copy()
    out[:, unstriped(offs4)] = np.tile(f64(wgo), (N // B, 1)) * y
    return out

@@ -1,0 +1,335 @@
+import math
+from contextlib import ExitStack
+
+import concourse.mybir as mybir
+
+K, T, S, H, N, M, T2, B = 1024, 4096, 1024, 1024, 512, 1024, 2048, 128
+FLOPS = 2 * K * H * S + 4 * H * N * M
+
+F32 = mybir.dt.float32
+BF16 = mybir.dt.bfloat16
+I32 = mybir.dt.int32
+U32 = mybir.dt.uint32
+U16 = mybir.dt.uint16
+U8 = mybir.dt.uint8
+FP8X4 = mybir.dt.float8_e4m3fn_x4
+FP4X4 = mybir.dt.float4_e2m1fn_x4
+ACT = mybir.ActivationFunctionType
+MULT = mybir.AluOpType.mult
+ADD = mybir.AluOpType.add
+
+P = 128
+BANK = 512
+PIECES = {0: [(0, 512), (512, 512)], 1: [(0, 256), (256, 256), (512, 256), (768, 256)]}
+
+
+def tile_list_seaweed_harvest_page_kernel(
+    tc, tab_words, tab_scales, offs, w1, gain, page0, offs2, wgs, offs3, steep, lift, w2, w3_words, w3_scales,
+    page1, offs4, wgo, out,
+):
+    nc = tc.nc
+    with ExitStack() as ctx:
+        held = ctx.enter_context(tc.tile_pool(name="held", bufs=1))
+        raws = ctx.enter_context(tc.tile_pool(name="raws", bufs=4))
+        pages = ctx.enter_context(tc.tile_pool(name="pages", bufs=3))
+        work = ctx.enter_context(tc.tile_pool(name="work", bufs=2))
+        psum = ctx.enter_context(tc.psum_pool(name="psum", bufs=8))
+
+        lists = [held.tile([P, 64], U16, name="list%d" % i) for i in range(4)]
+
+        def entries(i, first, count):
+            if count == 1024:
+                return lists[i][:]
+            return lists[i][:, first // 16 : (first + count) // 16]
+
+        def load_rows(w, a, cols):
+            raw = raws.tile([P, 4, BANK], F32, name="raw", tag="raw")
+            nc.sync.dma_start(raw[:], w[512 * a : 512 * a + 512, cols].rearrange("(p j) c -> p j c", j=4))
+            return raw
+
+        page_rows = page0.rearrange("(b p t) c -> b t p c", b=2, t=4)
+
+        def load_page(s):
+            page = pages.tile([P, T2], F32, name="page", tag="page")
+            nc.sync.dma_start(page[:], page_rows[s // 4, s % 4])
+            return page
+
+        wgs_rows = wgs.rearrange("(q t) j -> q t j", t=4)
+
+        def load_wgs(t0, t1):
+            tile = held.tile([P, t1 - t0, S], F32, name="wgs%d" % t0)
+            for quad in (0, 2, 1, 3):
+                nc.sync.dma_start(tile[32 * quad : 32 * quad + 32], wgs_rows[:, t0:t1, :])
+            return [tile[:, t, :] for t in range(t1 - t0)]
+
+        def load_vec(vec, name):
+            tile = held.tile([P, 2, 4], F32, name=name)
+            nc.sync.dma_start(tile[:], vec.rearrange("(b p t) -> p b t", b=2, t=4))
+            return tile
+
+        def quantize(grouped, width, name, scales=None):
+            codes = held.tile([P, width], U32, name=name + "_codes", align_bytes=64)
+            if scales is None:
+                scales = held.tile([P, width], U8, name=name + "_scales", align_bytes=64)[:]
+            nc.vector.quantize_mx(out=codes[:].bitcast(FP8X4), scales=scales, in_=grouped[:])
+            return codes, scales
+
+        def new_grouped(width):
+            if width == BANK:
+                return work.tile([P, 4 * width], BF16, name="grouped", tag="grouped", bufs=6, align_bytes=64)
+            return work.tile([P, 4 * width], BF16, name="quarter", tag="quarter", bufs=4, align_bytes=64)
+
+        def interleave(src, width):
+            grouped = new_grouped(width)
+            nc.scalar.copy(
+                grouped[:].rearrange("p (c i t) -> p c t i", i=4, t=4),
+                src.rearrange("p t (c i) -> p c t i", i=4),
+            )
+            return grouped
+
+        def cast_w1(raw):
+            grouped = new_grouped(BANK)
+            nc.scalar.copy(
+                grouped[:].rearrange("p (t m j) -> p m t j", t=4, j=4),
+                raw[:].rearrange("p j (m t) -> p m t j", t=4),
+            )
+            return grouped
+
+        zero_in = held.tile([P, 1], F32, name="zero_in")
+        zero = held.tile([P, 1], F32, name="zero")
+        nc.vector.memset(zero_in[:], 0.0)
+        nc.scalar.activation(zero[:], zero_in[:], ACT.Silu)
+
+        tab_plane = held.tile([P, T], U8, name="tab_plane", tag="plane_then_words", align_bytes=64)
+        nc.vector.memset(tab_plane[:].bitcast(I32), 0)
+        for quad in range(4):
+            nc.gpsimd.dma_start(
+                tab_plane[32 * quad : 32 * quad + 8, :].bitcast(I32),
+                tab_scales[:, 4 * quad : 4 * quad + 4, :].bitcast(I32),
+            )
+        w3_plane = held.tile([P, 2, N], U8, name="w3_plane", align_bytes=64)
+        nc.vector.memset(w3_plane[:].rearrange("p a n -> p (a n)").bitcast(I32), 0)
+
+        with tc.tile_pool(name="table", bufs=1) as table:
+            tab_tiles = [table.tile([P, T], I32, name="tab%d" % a, align_bytes=64) for a in range(2)]
+
+            def load_tab(a):
+                nc.sync.dma_start(tab_tiles[a][:], tab_words[a].rearrange("p t i -> p (t i)").bitcast(I32))
+
+            nc.sync.dma_start(lists[0][:], offs)
+            load_tab(0)
+            w1_raw = {(a, 0): load_rows(w1, a, slice(0, 512)) for a in range(2)}
+            load_tab(1)
+            gain_sb = load_vec(gain, "gain_sb")
+            nc.sync.dma_start(lists[1][:], offs2)
+            wgs_sb = load_wgs(0, 1)
+            page_sb = {0: load_page(0)}
+            nc.sync.dma_start(lists[2][:], offs3)
+            steep_sb = load_vec(steep, "steep_sb")
+            lift_sb = load_vec(lift, "lift_sb")
+            wgs_sb = wgs_sb + load_wgs(1, 2)
+            page_sb[1] = load_page(1)
+            for a in range(2):
+                w1_raw[a, 1] = load_rows(w1, a, slice(512, 1024))
+            wgs_sb = wgs_sb + load_wgs(2, 4)
+            page_sb[2] = load_page(2)
+
+            v_words = [held.tile([P, S], U32, name="v0", align_bytes=64)]
+            nc.vector.tensor_copy(v_words[0][:], tab_tiles[0][:].bitcast(U32).indirect(entries(0, 0, S)))
+            v_plane = held.tile([P, S], U8, name="v_plane", align_bytes=64)
+            nc.vector.tensor_copy(v_plane[:], tab_plane[:].indirect(entries(0, 0, S)))
+            w1_q = {}
+            for a in range(2):
+                w1_q[a, 0] = quantize(cast_w1(w1_raw[a, 0]), BANK, "w1_%d0" % a)
+            v_words.append(held.tile([P, S], U32, name="v1", tag="plane_then_words", align_bytes=64))
+            for c0 in (0, BANK):
+                nc.vector.tensor_copy(
+                    v_words[1][:, c0 : c0 + BANK], tab_tiles[1][:].bitcast(U32).indirect(entries(0, c0, BANK))
+                )
+        picked = ctx.enter_context(tc.tile_pool(name="picked", bufs=1))
+
+        half_steep = held.tile([P, 2, 4], F32, name="half_steep")
+        neg_half_lift = held.tile([P, 2, 4], F32, name="neg_half_lift")
+        nc.scalar.activation(half_steep[:], steep_sb[:], ACT.Copy, scale=0.5)
+        nc.scalar.activation(neg_half_lift[:], lift_sb[:], ACT.Copy, scale=-0.5)
+
+        scratch = held.tile([P, 2, BANK], F32, name="scratch")
+        uses = []
+
+        def next_scratch(count):
+            uses.append(count)
+            return scratch[:, len(uses) % 2, 0:count]
+
+        h_sb = {}
+
+        def features(s):
+            b, t = divmod(s, 4)
+            h = held.tile([P, S], F32, name="h%d" % s, tag="h%d" % (s % 2), align_bytes=64)
+            for half in range(2):
+                cols = slice(half * BANK, (half + 1) * BANK)
+                bank = psum.tile([P, BANK], F32, name="bank", tag="bank")
+                for a in range(2):
+                    codes, scales = w1_q[a, b]
+                    nc.tensor.matmul_mx(
+                        out=bank[:],
+                        lhsT=codes[:, t * P : (t + 1) * P].bitcast(FP8X4),
+                        lhsT_scale=scales[:, t * P : (t + 1) * P],
+                        rhs=v_words[a][:, cols].bitcast(FP8X4),
+                        rhs_scale=v_plane[4 * a : P, cols],
+                        start=(a == 0),
+                        stop=(a == 1),
+                    )
+                size = next_scratch(BANK)
+                nc.scalar.activation(size, bank[:], ACT.Abs, bias=zero[:])
+                cos = work.tile([P, BANK], F32, name="cos", tag="cos", bufs=4)
+                nc.scalar.activation(cos[:], size, ACT.Sin, scale=-1.0, bias=math.pi / 2)
+                nc.vector.scalar_tensor_tensor(h[:, cols], bank[:], gain_sb[:, b, t : t + 1], cos[:], MULT, MULT)
+            h_sb[s] = h
+
+        def put(s):
+            step = BANK if s == 0 else S
+            for c0 in range(0, S, step):
+                nc.vector.tensor_tensor(
+                    page_sb[s][:].indirect(entries(1, c0, step)),
+                    h_sb[s][:, c0 : c0 + step],
+                    wgs_sb[s % 4][:, c0 : c0 + step],
+                    MULT,
+                )
+
+        x_sb, f_sb, x_grouped, f_grouped, x_q, f_q = {}, {}, {}, {}, {}, {}
+
+        def recall(s, first, count):
+            b, t = divmod(s, 4)
+            if t == 0:
+                x_sb[b, first] = picked.tile([P, 4, count], F32, name="x%d_%d" % (b, first))
+                f_sb[b, first] = held.tile(
+                    [P, 4, count], BF16, name="f%d_%d" % (b, first), tag="f%d" % first, align_bytes=64
+                )
+            nc.vector.tensor_copy(x_sb[b, first][:, t, :], page_sb[s][:].indirect(entries(2, first, count)))
+
+        def squash(s, first, count):
+            b, t = divmod(s, 4)
+            tanh = next_scratch(count)
+            nc.scalar.activation(
+                tanh, x_sb[b, first][:, t, :], ACT.Tanh, scale=half_steep[:, b, t : t + 1], bias=zero[:]
+            )
+            factor = neg_half_lift[:, b, t : t + 1]
+            nc.scalar.activation(f_sb[b, first][:, t, :], tanh, ACT.Identity, scale=factor, bias=factor)
+
+        w2_grouped, w2_q = {}, {}
+        w3_sb = held.tile([P, 2, 2 * N], U8, name="w3_sb", align_bytes=64)
+        wgo_sb = held.tile([P, M], F32, name="wgo_sb")
+        out_sb = {}
+
+        features(0)
+        put(0)
+        features(1)
+        for s in range(8):
+            if s > 0:
+                put(s)
+            if s == 1:
+                for a in range(2):
+                    w1_q[a, 1] = quantize(cast_w1(w1_raw[a, 1]), BANK, "w1_%d1" % a)
+            if s + 2 < 8:
+                features(s + 2)
+            for first, count in PIECES[s // 4]:
+                recall(s, first, count)
+            if s < 7:
+                for first, count in PIECES[s // 4]:
+                    squash(s, first, count)
+            if s + 3 < 8:
+                page_sb[s + 3] = load_page(s + 3)
+            if s in (1, 2):
+                w2_grouped[s - 1] = interleave(load_rows(w2, s - 1, slice(0, N))[:], N)
+            if s == 3:
+                for first, count in PIECES[0]:
+                    f_grouped[0, first] = interleave(f_sb[0, first][:], count)
+            if s in (4, 5):
+                first, count = PIECES[0][s - 4]
+                x_grouped[0, first] = interleave(x_sb[0, first][:], count)
+            if s == 2:
+                nc.sync.dma_start(w3_sb[:].bitcast(I32), w3_words.rearrange("a p c -> p a c").bitcast(I32))
+                for quad in range(4):
+                    nc.sync.dma_start(
+                        w3_plane[32 * quad : 32 * quad + 4].bitcast(I32),
+                        w3_scales[:, 4 * quad : 4 * quad + 4, :].rearrange("a r n -> r a n").bitcast(I32),
+                    )
+                nc.sync.dma_start(lists[3][:], offs4)
+                nc.sync.dma_start(wgo_sb[:], wgo)
+            if s >= 4:
+                n = s - 4
+                out_sb[n] = raws.tile([P, T2], F32, name="harvest", tag="raw")
+                nc.sync.dma_start(out_sb[n][:], page1[n * P : (n + 1) * P, :])
+
+        early = held.tile([P, 4, BANK], U8, name="early_planes", tag="h1", align_bytes=64)
+        for a in range(2):
+            w2_q[a] = quantize(w2_grouped[a], N, "w2_%d" % a, early[:, a, :])
+        x_q[0, 0] = quantize(x_grouped[0, 0], BANK, "x0_0", early[:, 2, :])
+        f_q[0, 0] = quantize(f_grouped[0, 0], BANK, "f0_0", early[:, 3, :])
+
+        def second_half(piece):
+            first, count = PIECES[1][piece]
+            squash(7, first, count)
+            xg = interleave(x_sb[1, first][:], count)
+            fg = interleave(f_sb[1, first][:], count)
+            x_q[1, first] = quantize(xg, count, "x1_%d" % first)
+            f_q[1, first] = quantize(fg, count, "f1_%d" % first)
+
+        def moving(table_q, b, first, count):
+            for (bb, f0), (codes, scales) in table_q.items():
+                if bb == b and f0 <= first and first + count <= f0 + codes.shape[1]:
+                    return codes[:, first - f0 : first - f0 + count], scales[:, first - f0 : first - f0 + count]
+            raise ValueError("no such piece")
+
+        def harvest(n, piece):
+            first, count = PIECES[1][piece]
+            bank = psum.tile([P, BANK], F32, name="bank", tag="bank")
+            rows = slice(n * P, (n + 1) * P)
+            width = BANK if count == BANK else P
+            for b in range(2):
+                codes, scales = moving(x_q, b, first, count)
+                nc.tensor.matmul_mx(
+                    out=bank[:, 0:count],
+                    lhsT=w2_q[b][0][:, rows].bitcast(FP8X4),
+                    lhsT_scale=w2_q[b][1][:, rows],
+                    rhs=codes.bitcast(FP8X4),
+                    rhs_scale=scales,
+                    start=(b == 0),
+                    stop=False,
+                )
+                for c0 in range(0, count, width):
+                    codes, scales = moving(f_q, b, first + c0, width)
+                    nc.tensor.matmul_mx(
+                        out=bank[:, c0 : c0 + width],
+                        lhsT=w3_sb[:, b, 2 * n * P : 2 * (n + 1) * P].bitcast(FP4X4),
+                        lhsT_scale=w3_plane[:, b, rows],
+                        rhs=codes.bitcast(FP8X4),
+                        rhs_scale=scales,
+                        start=False,
+                        stop=(b == 1 and c0 + width == count),
+                    )
+            y = work.tile([P, BANK], F32, name="y", tag="cos", bufs=4)
+            nc.scalar.copy(y[:, 0:count], bank[:, 0:count])
+            nc.vector.tensor_tensor(
+                out_sb[n][:].indirect(entries(3, first, count)), y[:, 0:count], wgo_sb[:, first : first + count], MULT
+            )
+            if piece == len(PIECES[1]) - 1:
+                nc.sync.dma_start(out[n * P : (n + 1) * P, :], out_sb[n][:])
+
+        second_half(0)
+        late = held.tile([P, 2, BANK], U8, name="late_planes", tag="f0", align_bytes=64)
+        x_q[0, BANK] = quantize(x_grouped[0, BANK], BANK, "x0_1", late[:, 0, :])
+        f_q[0, BANK] = quantize(f_grouped[0, BANK], BANK, "f0_1", late[:, 1, :])
+        harvest(0, 0)
+        second_half(1)
+        harvest(1, 0)
+        harvest(2, 0)
+        second_half(2)
+        for n in range(3):
+            harvest(n, 1)
+        second_half(3)
+        for n in range(3):
+            harvest(n, 2)
+            harvest(n, 3)
+        for piece in range(4):
+            harvest(3, piece)

@@ -3,7 +3,7 @@ from contextlib import ExitStack
 
 import concourse.mybir as mybir
 
-K, T, S, H, N, M, T2, B = 1024, 4096, 1024, 1024, 512, 1024, 2048, 128
+K, T, S, H, N, M, T2 = 1024, 4096, 1024, 1024, 512, 1024, 2048
 FLOPS = 2 * K * H * S + 4 * H * N * M
 
 F32 = mybir.dt.float32
@@ -20,7 +20,12 @@ ADD = mybir.AluOpType.add
 
 P = 128
 BANK = 512
-PIECES = {0: [(0, 512), (512, 512)], 1: [(0, 256), (256, 256), (512, 256), (768, 256)]}
+KIB = 1024
+SLICES = 8
+PAGE_SLOTS = 3
+HALVES = [(0, BANK), (BANK, BANK)]
+QUARTERS = [(first, BANK // 2) for first in range(0, S, BANK // 2)]
+RUNS = [HALVES, [QUARTERS[0], QUARTERS[1], HALVES[1]]]
 
 
 def tile_list_seaweed_harvest_page_kernel(
@@ -30,77 +35,83 @@ def tile_list_seaweed_harvest_page_kernel(
     nc = tc.nc
     with ExitStack() as ctx:
         held = ctx.enter_context(tc.tile_pool(name="held", bufs=1))
-        raws = ctx.enter_context(tc.tile_pool(name="raws", bufs=4))
-        pages = ctx.enter_context(tc.tile_pool(name="pages", bufs=3))
-        work = ctx.enter_context(tc.tile_pool(name="work", bufs=2))
+        raws = ctx.enter_context(tc.tile_pool(name="raws", bufs=2))
+        pages = ctx.enter_context(tc.tile_pool(name="pages", bufs=1))
+        work = ctx.enter_context(tc.tile_pool(name="work", bufs=4))
+        table = ctx.enter_context(tc.tile_pool(name="table", bufs=1))
         psum = ctx.enter_context(tc.psum_pool(name="psum", bufs=8))
 
-        lists = [held.tile([P, 64], U16, name="list%d" % i) for i in range(4)]
+        idx, idx2, idx3, idx4 = [held.tile([P, S // 16], U16, name="list%d" % i) for i in range(4)]
 
-        def entries(i, first, count):
-            if count == 1024:
-                return lists[i][:]
-            return lists[i][:, first // 16 : (first + count) // 16]
+        def entries(tile, first, count):
+            return tile[:, first // 16 : (first + count) // 16]
 
-        def load_rows(w, a, cols):
-            raw = raws.tile([P, 4, BANK], F32, name="raw", tag="raw")
-            nc.sync.dma_start(raw[:], w[512 * a : 512 * a + 512, cols].rearrange("(p j) c -> p j c", j=4))
+        def load_rows(w, a, first_col, pool, tag):
+            raw = pool.tile([P, 4, BANK], F32, name="raw", tag=tag)
+            rows = w[BANK * a : BANK * (a + 1), first_col : first_col + BANK]
+            nc.sync.dma_start(raw[:], rows.rearrange("(p j) c -> p j c", j=4))
             return raw
 
-        page_rows = page0.rearrange("(b p t) c -> b t p c", b=2, t=4)
+        def page_slot(shape, name, s):
+            return pages.tile(shape, F32, name=name, offset=4 * T2 * (s % PAGE_SLOTS))
+
+        page_sb = {}
 
         def load_page(s):
-            page = pages.tile([P, T2], F32, name="page", tag="page")
-            nc.sync.dma_start(page[:], page_rows[s // 4, s % 4])
-            return page
+            page_sb[s] = page_slot([P, T2], "page%d" % s, s)
+            nc.sync.dma_start(page_sb[s][:], page0.rearrange("(b p t) c -> b t p c", b=2, t=4)[s // 4, s % 4])
 
-        wgs_rows = wgs.rearrange("(q t) j -> q t j", t=4)
+        wgs_sb = {}
 
-        def load_wgs(t0, t1):
-            tile = held.tile([P, t1 - t0, S], F32, name="wgs%d" % t0)
+        def load_wgs(t0, t1, first, count):
+            tile = held.tile([P, t1 - t0, count], F32, name="wgs%d_%d" % (t0, first))
+            rows = wgs.rearrange("(q t) j -> q t j", t=4)[:, t0:t1, first : first + count]
             for quad in (0, 2, 1, 3):
-                nc.sync.dma_start(tile[32 * quad : 32 * quad + 32], wgs_rows[:, t0:t1, :])
-            return [tile[:, t, :] for t in range(t1 - t0)]
+                nc.sync.dma_start(tile[32 * quad : 32 * quad + 32], rows)
+            for t in range(t0, t1):
+                for c0 in range(0, count, BANK):
+                    wgs_sb[t, (first + c0) // BANK] = tile[:, t - t0, c0 : c0 + BANK]
 
-        def load_vec(vec, name):
+        def load_by_slice(vec, name):
             tile = held.tile([P, 2, 4], F32, name=name)
             nc.sync.dma_start(tile[:], vec.rearrange("(b p t) -> p b t", b=2, t=4))
             return tile
 
-        def quantize(grouped, width, name, scales=None):
-            codes = held.tile([P, width], U32, name=name + "_codes", align_bytes=64)
-            if scales is None:
-                scales = held.tile([P, width], U8, name=name + "_scales", align_bytes=64)[:]
-            nc.vector.quantize_mx(out=codes[:].bitcast(FP8X4), scales=scales, in_=grouped[:])
-            return codes, scales
-
-        def new_grouped(width):
+        def new_grouped(width, tag):
+            if tag:
+                return held.tile([P, 4 * width], BF16, name="grouped", tag=tag, align_bytes=64)
             if width == BANK:
-                return work.tile([P, 4 * width], BF16, name="grouped", tag="grouped", bufs=6, align_bytes=64)
-            return work.tile([P, 4 * width], BF16, name="quarter", tag="quarter", bufs=4, align_bytes=64)
+                return work.tile([P, 4 * width], BF16, name="grouped", tag="grouped", bufs=5, align_bytes=64)
+            return work.tile([P, 4 * width], BF16, name="quarter", tag="quarter", bufs=3, align_bytes=64)
 
-        def interleave(src, width):
-            grouped = new_grouped(width)
+        def interleave(src, tag=""):
+            grouped = new_grouped(src.shape[2], tag)
             nc.scalar.copy(
-                grouped[:].rearrange("p (c i t) -> p c t i", i=4, t=4),
-                src.rearrange("p t (c i) -> p c t i", i=4),
+                grouped[:].rearrange("p (c i j) -> p c j i", i=4, j=4), src.rearrange("p j (c i) -> p c j i", i=4)
             )
             return grouped
 
-        def cast_w1(raw):
-            grouped = new_grouped(BANK)
+        def interleave_dealt(raw, tag):
+            grouped = new_grouped(BANK, tag)
             nc.scalar.copy(
-                grouped[:].rearrange("p (t m j) -> p m t j", t=4, j=4),
-                raw[:].rearrange("p j (m t) -> p m t j", t=4),
+                grouped[:].rearrange("p (t m j) -> p m t j", t=4, j=4), raw[:].rearrange("p j (m t) -> p m t j", t=4)
             )
             return grouped
+
+        def new_plane(width, name):
+            return held.tile([P, width], U8, name=name, align_bytes=64)[:]
+
+        def quantize(grouped, plane, name):
+            codes = held.tile([P, plane.shape[1]], U32, name=name, align_bytes=64)
+            nc.vector.quantize_mx(out=codes[:].bitcast(FP8X4), scales=plane, in_=grouped[:])
+            return codes, plane
 
         zero_in = held.tile([P, 1], F32, name="zero_in")
         zero = held.tile([P, 1], F32, name="zero")
         nc.vector.memset(zero_in[:], 0.0)
         nc.scalar.activation(zero[:], zero_in[:], ACT.Silu)
 
-        tab_plane = held.tile([P, T], U8, name="tab_plane", tag="plane_then_words", align_bytes=64)
+        tab_plane = table.tile([P, T], U8, name="tab_plane", align_bytes=64, offset=33 * KIB)
         nc.vector.memset(tab_plane[:].bitcast(I32), 0)
         for quad in range(4):
             nc.gpsimd.dma_start(
@@ -110,143 +121,195 @@ def tile_list_seaweed_harvest_page_kernel(
         w3_plane = held.tile([P, 2, N], U8, name="w3_plane", align_bytes=64)
         nc.vector.memset(w3_plane[:].rearrange("p a n -> p (a n)").bitcast(I32), 0)
 
-        with tc.tile_pool(name="table", bufs=1) as table:
-            tab_tiles = [table.tile([P, T], I32, name="tab%d" % a, align_bytes=64) for a in range(2)]
+        nc.sync.dma_start(idx[:], offs)
+        w1_raw = {(a, 0): load_rows(w1, a, 0, raws, "raw") for a in range(2)}
+        tab_sb = []
+        for a, offset in enumerate((17 * KIB, 0)):
+            tab_sb.append(table.tile([P, T], I32, name="tab%d" % a, align_bytes=64, offset=offset))
+            nc.sync.dma_start(tab_sb[a][:], tab_words[a].rearrange("p t i -> p (t i)").bitcast(I32))
+        gain_sb = load_by_slice(gain, "gain_sb")
+        nc.sync.dma_start(idx2[:], offs2)
+        load_wgs(0, 1, *HALVES[0])
+        load_page(0)
+        load_wgs(0, 1, *HALVES[1])
+        nc.sync.dma_start(idx3[:], offs3)
+        steep_sb = load_by_slice(steep, "steep_sb")
+        lift_sb = load_by_slice(lift, "lift_sb")
+        w1_raw[0, 1] = load_rows(w1, 0, BANK, held, "w1_w2_out2")
+        w1_raw[1, 1] = load_rows(w1, 1, BANK, held, "w1_scratch")
+        load_wgs(1, 2, 0, S)
+        load_page(1)
+        load_wgs(2, 4, 0, S)
+        load_page(2)
 
-            def load_tab(a):
-                nc.sync.dma_start(tab_tiles[a][:], tab_words[a].rearrange("p t i -> p (t i)").bitcast(I32))
-
-            nc.sync.dma_start(lists[0][:], offs)
-            load_tab(0)
-            w1_raw = {(a, 0): load_rows(w1, a, slice(0, 512)) for a in range(2)}
-            load_tab(1)
-            gain_sb = load_vec(gain, "gain_sb")
-            nc.sync.dma_start(lists[1][:], offs2)
-            wgs_sb = load_wgs(0, 1)
-            page_sb = {0: load_page(0)}
-            nc.sync.dma_start(lists[2][:], offs3)
-            steep_sb = load_vec(steep, "steep_sb")
-            lift_sb = load_vec(lift, "lift_sb")
-            wgs_sb = wgs_sb + load_wgs(1, 2)
-            page_sb[1] = load_page(1)
-            for a in range(2):
-                w1_raw[a, 1] = load_rows(w1, a, slice(512, 1024))
-            wgs_sb = wgs_sb + load_wgs(2, 4)
-            page_sb[2] = load_page(2)
-
-            v_words = [held.tile([P, S], U32, name="v0", align_bytes=64)]
-            nc.vector.tensor_copy(v_words[0][:], tab_tiles[0][:].bitcast(U32).indirect(entries(0, 0, S)))
-            v_plane = held.tile([P, S], U8, name="v_plane", align_bytes=64)
-            nc.vector.tensor_copy(v_plane[:], tab_plane[:].indirect(entries(0, 0, S)))
-            w1_q = {}
-            for a in range(2):
-                w1_q[a, 0] = quantize(cast_w1(w1_raw[a, 0]), BANK, "w1_%d0" % a)
-            v_words.append(held.tile([P, S], U32, name="v1", tag="plane_then_words", align_bytes=64))
-            for c0 in (0, BANK):
-                nc.vector.tensor_copy(
-                    v_words[1][:, c0 : c0 + BANK], tab_tiles[1][:].bitcast(U32).indirect(entries(0, c0, BANK))
-                )
-        picked = ctx.enter_context(tc.tile_pool(name="picked", bufs=1))
+        w1_q = {}
+        for a, tag in enumerate(("", "w1_words")):
+            w1_q[a, 0] = quantize(interleave_dealt(w1_raw[a, 0], tag), new_plane(BANK, "w1s%d0" % a), "w1q%d0" % a)
+        v0 = held.tile([P, S], U32, name="v0", tag="w1_words", align_bytes=64)
+        nc.vector.tensor_copy(v0[:], tab_sb[0][:].bitcast(U32).indirect(idx[:]))
+        v_plane = table.tile([P, S], U8, name="v_plane", align_bytes=64, offset=32 * KIB)
+        nc.vector.tensor_copy(v_plane[:], tab_plane[:].indirect(idx[:]))
+        v_words = {}
+        for half, (first, count) in enumerate(HALVES):
+            v1 = table.tile([P, count], U32, name="v1_%d" % half, align_bytes=64, offset=33 * KIB + 4 * first)
+            nc.vector.tensor_copy(v1[:], tab_sb[1][:].bitcast(U32).indirect(entries(idx, first, count)))
+            v_words[0, half], v_words[1, half] = v0[:, first : first + count], v1[:]
 
         half_steep = held.tile([P, 2, 4], F32, name="half_steep")
         neg_half_lift = held.tile([P, 2, 4], F32, name="neg_half_lift")
-        nc.scalar.activation(half_steep[:], steep_sb[:], ACT.Copy, scale=0.5)
-        nc.scalar.activation(neg_half_lift[:], lift_sb[:], ACT.Copy, scale=-0.5)
+        nc.gpsimd.tensor_scalar(half_steep[:], steep_sb[:], 0.5, 0.0, MULT, ADD)
+        nc.gpsimd.tensor_scalar(neg_half_lift[:], lift_sb[:], -0.5, 0.0, MULT, ADD)
 
-        scratch = held.tile([P, 2, BANK], F32, name="scratch")
-        uses = []
+        scratch = [held.tile([P, 2, BANK], F32, name="scratch", tag="scratch_w2_out3")]
+        scratch_uses = []
 
         def next_scratch(count):
-            uses.append(count)
-            return scratch[:, len(uses) % 2, 0:count]
+            scratch_uses.append(count)
+            return scratch[-1][:, len(scratch_uses) % 2, 0:count]
+
+        def product(s, first, count):
+            b, t = divmod(s, 4)
+            half, inner = divmod(first, BANK)
+            bank = psum.tile([P, BANK], F32, name="bank", tag="bank")[:, 0:count]
+            for a in range(2):
+                codes, plane = w1_q[a, b]
+                nc.tensor.matmul_mx(
+                    out=bank,
+                    lhsT=codes[:, t * P : (t + 1) * P].bitcast(FP8X4),
+                    lhsT_scale=plane[:, t * P : (t + 1) * P],
+                    rhs=v_words[a, half][:, inner : inner + count].bitcast(FP8X4),
+                    rhs_scale=v_plane[4 * a : P, first : first + count],
+                    start=(a == 0),
+                    stop=(a == 1),
+                )
+            return bank
+
+        def ring(tag, count):
+            return work.tile([P, BANK], F32, name=tag, tag=tag)[:, 0:count]
+
+        def weight_buffer(i):
+            return held.tile([P, BANK], F32, name="before_weights", tag="weights%d" % i, align_bytes=64)[:]
+
+        def cosine(cos, size):
+            nc.scalar.activation(cos, size, ACT.Sin, scale=-1.0, bias=math.pi / 2)
+
+        def gain_of(s):
+            return gain_sb[:, s // 4, s % 4 : s % 4 + 1]
+
+        def wgs_of(s, first, count):
+            half, inner = divmod(first, BANK)
+            return wgs_sb[s % 4, half][:, inner : inner + count]
+
+        factors = {}
+
+        def make_factors(s, first, count):
+            bank = product(s, first, count)
+            size = weight_buffer(first // BANK) if s == 1 else next_scratch(count)
+            cos = weight_buffer(s - 3) if s in (3, 4) and first == 0 else ring("cos", count)
+            gained = ring("gained", count)
+            nc.scalar.activation(size, bank, ACT.Abs, bias=zero[:])
+            nc.scalar.activation(gained, bank, ACT.Copy, scale=gain_of(s))
+            cosine(cos, size)
+            factors[s, first] = gained, cos
 
         h_sb = {}
 
-        def features(s):
-            b, t = divmod(s, 4)
-            h = held.tile([P, S], F32, name="h%d" % s, tag="h%d" % (s % 2), align_bytes=64)
-            for half in range(2):
-                cols = slice(half * BANK, (half + 1) * BANK)
-                bank = psum.tile([P, BANK], F32, name="bank", tag="bank")
-                for a in range(2):
-                    codes, scales = w1_q[a, b]
-                    nc.tensor.matmul_mx(
-                        out=bank[:],
-                        lhsT=codes[:, t * P : (t + 1) * P].bitcast(FP8X4),
-                        lhsT_scale=scales[:, t * P : (t + 1) * P],
-                        rhs=v_words[a][:, cols].bitcast(FP8X4),
-                        rhs_scale=v_plane[4 * a : P, cols],
-                        start=(a == 0),
-                        stop=(a == 1),
-                    )
-                size = next_scratch(BANK)
-                nc.scalar.activation(size, bank[:], ACT.Abs, bias=zero[:])
-                cos = work.tile([P, BANK], F32, name="cos", tag="cos", bufs=4)
-                nc.scalar.activation(cos[:], size, ACT.Sin, scale=-1.0, bias=math.pi / 2)
-                nc.vector.scalar_tensor_tensor(h[:, cols], bank[:], gain_sb[:, b, t : t + 1], cos[:], MULT, MULT)
-            h_sb[s] = h
+        def new_h(s):
+            h_sb[s] = held.tile([P, S], F32, name="h%d" % s, tag="h%d" % (s % 2), align_bytes=64)
 
-        def put(s):
-            step = BANK if s == 0 else S
-            for c0 in range(0, S, step):
-                nc.vector.tensor_tensor(
-                    page_sb[s][:].indirect(entries(1, c0, step)),
-                    h_sb[s][:, c0 : c0 + step],
-                    wgs_sb[s % 4][:, c0 : c0 + step],
-                    MULT,
-                )
+        def multiply(s, runs, weighted):
+            base = runs[0][0]
+            for first, count in runs:
+                part = weighted[:, first - base : first - base + count]
+                nc.gpsimd.tensor_tensor(part, factors[s, first][1], wgs_of(s, first, count), MULT)
+            for first, count in runs:
+                part = weighted[:, first - base : first - base + count]
+                nc.gpsimd.tensor_tensor(h_sb[s][:, first : first + count], factors[s, first][0], part, MULT)
 
-        x_sb, f_sb, x_grouped, f_grouped, x_q, f_q = {}, {}, {}, {}, {}, {}
+        def put(s, first, count):
+            nc.vector.tensor_copy(
+                page_sb[s][:].indirect(entries(idx2, first, count)), h_sb[s][:, first : first + count]
+            )
 
-        def recall(s, first, count):
+        x_sb, f_sb = {}, {}
+
+        def recall(s):
             b, t = divmod(s, 4)
             if t == 0:
-                x_sb[b, first] = picked.tile([P, 4, count], F32, name="x%d_%d" % (b, first))
-                f_sb[b, first] = held.tile(
-                    [P, 4, count], BF16, name="f%d_%d" % (b, first), tag="f%d" % first, align_bytes=64
+                x_sb[b] = table.tile([P, 4, M], F32, name="x%d" % b, align_bytes=64, offset=16 * KIB * b)
+                for first, count in RUNS[b]:
+                    f_sb[b, first] = held.tile(
+                        [P, 4, count], BF16, name="f%d_%d" % (b, first), tag="f%d" % first, align_bytes=64
+                    )
+            for first, count in RUNS[b] if s == SLICES - 1 else [(0, M)]:
+                nc.vector.tensor_copy(
+                    x_sb[b][:, t, first : first + count], page_sb[s][:].indirect(entries(idx3, first, count))
                 )
-            nc.vector.tensor_copy(x_sb[b, first][:, t, :], page_sb[s][:].indirect(entries(2, first, count)))
 
         def squash(s, first, count):
             b, t = divmod(s, 4)
             tanh = next_scratch(count)
             nc.scalar.activation(
-                tanh, x_sb[b, first][:, t, :], ACT.Tanh, scale=half_steep[:, b, t : t + 1], bias=zero[:]
+                tanh, x_sb[b][:, t, first : first + count], ACT.Tanh, scale=half_steep[:, b, t : t + 1], bias=zero[:]
             )
             factor = neg_half_lift[:, b, t : t + 1]
             nc.scalar.activation(f_sb[b, first][:, t, :], tanh, ACT.Identity, scale=factor, bias=factor)
 
-        w2_grouped, w2_q = {}, {}
+        new_h(0)
+        for first, count in QUARTERS[:2]:
+            bank = product(0, first, count)
+            size, cos, unweighted = next_scratch(count), ring("cos", count), ring("gained", count)
+            nc.scalar.activation(size, bank, ACT.Abs, bias=zero[:])
+            cosine(cos, size)
+            nc.vector.scalar_tensor_tensor(unweighted, bank, gain_of(0), cos, MULT, MULT)
+            nc.vector.tensor_tensor(h_sb[0][:, first : first + count], unweighted, wgs_of(0, first, count), MULT)
+            put(0, first, count)
+        for first, count in QUARTERS[2:]:
+            make_factors(0, first, count)
+        multiply(0, QUARTERS[2:], table.tile([P, BANK], F32, name="weighted0", offset=20 * KIB))
+        for first, count in QUARTERS[2:]:
+            put(0, first, count)
+        for first, count in HALVES:
+            make_factors(1, first, count)
+        new_h(1)
+        multiply(1, HALVES, table.tile([P, S], F32, name="weighted1", offset=24 * KIB))
+        for a in range(2):
+            grouped = interleave_dealt(w1_raw[a, 1], "weights%d" % a)
+            w1_q[a, 1] = quantize(grouped, new_plane(BANK, "w1s%d1" % a), "w1q%d1" % a)
+        scratch.append(held.tile([P, 2, BANK], F32, name="scratch", tag="w1_scratch"))
+        for first, count in HALVES:
+            make_factors(2, first, count)
+
+        w2_tags = ("w1_w2_out2", "scratch_w2_out3")
+        w2_grouped, f_grouped, x_grouped, out_sb = {}, {}, {}, {}
         w3_sb = held.tile([P, 2, 2 * N], U8, name="w3_sb", align_bytes=64)
         wgo_sb = held.tile([P, M], F32, name="wgo_sb")
-        out_sb = {}
 
-        features(0)
-        put(0)
-        features(1)
-        for s in range(8):
+        for s in range(SLICES):
+            b, t = divmod(s, 4)
             if s > 0:
-                put(s)
-            if s == 1:
-                for a in range(2):
-                    w1_q[a, 1] = quantize(cast_w1(w1_raw[a, 1]), BANK, "w1_%d1" % a)
-            if s + 2 < 8:
-                features(s + 2)
-            for first, count in PIECES[s // 4]:
-                recall(s, first, count)
-            if s < 7:
-                for first, count in PIECES[s // 4]:
+                put(s, 0, S)
+            recall(s)
+            if s + 2 < SLICES:
+                new_h(s + 2)
+                multiply(s + 2, HALVES, page_slot([P, S], "weighted%d" % (s + 2), s))
+            if s + PAGE_SLOTS < SLICES:
+                load_page(s + PAGE_SLOTS)
+            if s < SLICES - 1:
+                for first, count in RUNS[b]:
                     squash(s, first, count)
-            if s + 3 < 8:
-                page_sb[s + 3] = load_page(s + 3)
+            if s + 3 < SLICES:
+                for first, count in HALVES:
+                    make_factors(s + 3, first, count)
             if s in (1, 2):
-                w2_grouped[s - 1] = interleave(load_rows(w2, s - 1, slice(0, N))[:], N)
+                w2_raw = load_rows(w2, s - 1, 0, held, w2_tags[s - 1])
+                w2_grouped[s - 1] = interleave(w2_raw[:], "weights%d" % (s - 1))
             if s == 3:
-                for first, count in PIECES[0]:
-                    f_grouped[0, first] = interleave(f_sb[0, first][:], count)
+                for first, count in HALVES:
+                    f_grouped[first] = interleave(f_sb[0, first][:])
             if s in (4, 5):
-                first, count = PIECES[0][s - 4]
-                x_grouped[0, first] = interleave(x_sb[0, first][:], count)
+                first, count = HALVES[s - 4]
+                x_grouped[first] = interleave(x_sb[0][:, :, first : first + count])
             if s == 2:
                 nc.sync.dma_start(w3_sb[:].bitcast(I32), w3_words.rearrange("a p c -> p a c").bitcast(I32))
                 for quad in range(4):
@@ -254,82 +317,75 @@ def tile_list_seaweed_harvest_page_kernel(
                         w3_plane[32 * quad : 32 * quad + 4].bitcast(I32),
                         w3_scales[:, 4 * quad : 4 * quad + 4, :].rearrange("a r n -> r a n").bitcast(I32),
                     )
-                nc.sync.dma_start(lists[3][:], offs4)
+                nc.sync.dma_start(idx4[:], offs4)
                 nc.sync.dma_start(wgo_sb[:], wgo)
-            if s >= 4:
-                n = s - 4
-                out_sb[n] = raws.tile([P, T2], F32, name="harvest", tag="raw")
-                nc.sync.dma_start(out_sb[n][:], page1[n * P : (n + 1) * P, :])
+            if b == 1:
+                pool, tag = (raws, "raw") if t < 2 else (held, w2_tags[t - 2])
+                out_sb[t] = pool.tile([P, T2], F32, name="harvest", tag=tag)
+                nc.sync.dma_start(out_sb[t][:], page1[t * P : (t + 1) * P, :])
 
-        early = held.tile([P, 4, BANK], U8, name="early_planes", tag="h1", align_bytes=64)
-        for a in range(2):
-            w2_q[a] = quantize(w2_grouped[a], N, "w2_%d" % a, early[:, a, :])
-        x_q[0, 0] = quantize(x_grouped[0, 0], BANK, "x0_0", early[:, 2, :])
-        f_q[0, 0] = quantize(f_grouped[0, 0], BANK, "f0_0", early[:, 3, :])
+        early = held.tile([P, 4, BANK], U8, name="early_planes", tag="h%d" % ((SLICES - 1) % 2), align_bytes=64)
+        w2_q = [quantize(w2_grouped[a], early[:, a, :], "w2q%d" % a) for a in range(2)]
+        x_q = {(0, 0): quantize(x_grouped[0], early[:, 2, :], "xq0_0")}
+        f_q = {(0, 0): quantize(f_grouped[0], early[:, 3, :], "fq0_0")}
 
-        def second_half(piece):
-            first, count = PIECES[1][piece]
-            squash(7, first, count)
-            xg = interleave(x_sb[1, first][:], count)
-            fg = interleave(f_sb[1, first][:], count)
-            x_q[1, first] = quantize(xg, count, "x1_%d" % first)
-            f_q[1, first] = quantize(fg, count, "f1_%d" % first)
+        def finish_f(first, count):
+            squash(SLICES - 1, first, count)
+            grouped = interleave(f_sb[1, first][:])
+            f_q[1, first] = quantize(grouped, new_plane(count, "fs1_%d" % first), "fq1_%d" % first)
 
-        def moving(table_q, b, first, count):
-            for (bb, f0), (codes, scales) in table_q.items():
-                if bb == b and f0 <= first and first + count <= f0 + codes.shape[1]:
-                    return codes[:, first - f0 : first - f0 + count], scales[:, first - f0 : first - f0 + count]
-            raise ValueError("no such piece")
+        def finish_x(first, count):
+            grouped = interleave(x_sb[1][:, :, first : first + count])
+            x_q[1, first] = quantize(grouped, new_plane(count, "xs1_%d" % first), "xq1_%d" % first)
 
-        def harvest(n, piece):
-            first, count = PIECES[1][piece]
+        def harvest(n, first, count):
             bank = psum.tile([P, BANK], F32, name="bank", tag="bank")
             rows = slice(n * P, (n + 1) * P)
-            width = BANK if count == BANK else P
-            for b in range(2):
-                codes, scales = moving(x_q, b, first, count)
+            passes = []
+            for b in (0, 1) if (n, first) == (0, 0) else (1, 0):
+                w2_b = w2_q[b][0][:, rows].bitcast(FP8X4), w2_q[b][1][:, rows]
+                w3_b = w3_sb[:, b, 2 * n * P : 2 * (n + 1) * P].bitcast(FP4X4), w3_plane[:, b, rows]
+                for start, size in RUNS[b]:
+                    low, high = max(first, start), min(first + count, start + size)
+                    if low < high:
+                        width = BANK if high - low == BANK else P
+                        passes.append((w2_b, x_q[b, start], low - start, low - first, high - low))
+                        for c0 in range(low, high, width):
+                            passes.append((w3_b, f_q[b, start], c0 - start, c0 - first, width))
+            for i, (weight, (codes, plane), src, dst, width) in enumerate(passes):
                 nc.tensor.matmul_mx(
-                    out=bank[:, 0:count],
-                    lhsT=w2_q[b][0][:, rows].bitcast(FP8X4),
-                    lhsT_scale=w2_q[b][1][:, rows],
-                    rhs=codes.bitcast(FP8X4),
-                    rhs_scale=scales,
-                    start=(b == 0),
-                    stop=False,
+                    out=bank[:, dst : dst + width],
+                    lhsT=weight[0],
+                    lhsT_scale=weight[1],
+                    rhs=codes[:, src : src + width].bitcast(FP8X4),
+                    rhs_scale=plane[:, src : src + width],
+                    start=(i == 0),
+                    stop=(i == len(passes) - 1),
                 )
-                for c0 in range(0, count, width):
-                    codes, scales = moving(f_q, b, first + c0, width)
-                    nc.tensor.matmul_mx(
-                        out=bank[:, c0 : c0 + width],
-                        lhsT=w3_sb[:, b, 2 * n * P : 2 * (n + 1) * P].bitcast(FP4X4),
-                        lhsT_scale=w3_plane[:, b, rows],
-                        rhs=codes.bitcast(FP8X4),
-                        rhs_scale=scales,
-                        start=False,
-                        stop=(b == 1 and c0 + width == count),
-                    )
-            y = work.tile([P, BANK], F32, name="y", tag="cos", bufs=4)
-            nc.scalar.copy(y[:, 0:count], bank[:, 0:count])
+            y = ring("cos", count)
+            nc.scalar.copy(y, bank[:, 0:count])
             nc.vector.tensor_tensor(
-                out_sb[n][:].indirect(entries(3, first, count)), y[:, 0:count], wgo_sb[:, first : first + count], MULT
+                out_sb[n][:].indirect(entries(idx4, first, count)), y, wgo_sb[:, first : first + count], MULT
             )
-            if piece == len(PIECES[1]) - 1:
-                nc.sync.dma_start(out[n * P : (n + 1) * P, :], out_sb[n][:])
+            if first + count == M:
+                nc.sync.dma_start(out[rows, :], out_sb[n][:])
 
-        second_half(0)
+        run0, run1, run2 = RUNS[1]
+        finish_f(*run0)
+        finish_x(*run0)
         late = held.tile([P, 2, BANK], U8, name="late_planes", tag="f0", align_bytes=64)
-        x_q[0, BANK] = quantize(x_grouped[0, BANK], BANK, "x0_1", late[:, 0, :])
-        f_q[0, BANK] = quantize(f_grouped[0, BANK], BANK, "f0_1", late[:, 1, :])
-        harvest(0, 0)
-        second_half(1)
-        harvest(1, 0)
-        harvest(2, 0)
-        second_half(2)
-        for n in range(3):
-            harvest(n, 1)
-        second_half(3)
-        for n in range(3):
-            harvest(n, 2)
-            harvest(n, 3)
-        for piece in range(4):
-            harvest(3, piece)
+        x_q[0, BANK] = quantize(x_grouped[BANK], late[:, 0, :], "xq0_1")
+        f_q[0, BANK] = quantize(f_grouped[BANK], late[:, 1, :], "fq0_1")
+        harvest(0, *run0)
+        finish_f(*run1)
+        finish_x(*run1)
+        harvest(1, *run0)
+        harvest(2, *run0)
+        harvest(0, *run1)
+        finish_f(*run2)
+        harvest(1, *run1)
+        harvest(2, *run1)
+        finish_x(*run2)
+        harvest(3, *HALVES[0])
+        for n in range(N // P):
+            harvest(n, *run2)

@@ -63,14 +63,13 @@ def tile_list_seaweed_harvest_page_kernel(
 
         wgs_sb = {}
 
-        def load_wgs(t0, t1, first, count):
-            tile = held.tile([P, t1 - t0, count], F32, name="wgs%d_%d" % (t0, first))
-            rows = wgs.rearrange("(q t) j -> q t j", t=4)[:, t0:t1, first : first + count]
+        def load_wgs(first_half, halves):
+            tile = held.tile([P, halves, BANK], F32, name="wgs%d" % first_half)
+            source = wgs.rearrange("(q t) (h j) -> q (t h) j", t=4, h=2)[:, first_half : first_half + halves, :]
             for quad in (0, 2, 1, 3):
-                nc.sync.dma_start(tile[32 * quad : 32 * quad + 32], rows)
-            for t in range(t0, t1):
-                for c0 in range(0, count, BANK):
-                    wgs_sb[t, (first + c0) // BANK] = tile[:, t - t0, c0 : c0 + BANK]
+                nc.sync.dma_start(tile[32 * quad : 32 * quad + 32], source)
+            for i in range(halves):
+                wgs_sb[divmod(first_half + i, 2)] = tile[:, i, :]
 
         def load_by_slice(vec, name):
             tile = held.tile([P, 2, 4], F32, name=name)
@@ -128,18 +127,17 @@ def tile_list_seaweed_harvest_page_kernel(
             tab_sb.append(table.tile([P, T], I32, name="tab%d" % a, align_bytes=64, offset=offset))
             nc.sync.dma_start(tab_sb[a][:], tab_words[a].rearrange("p t i -> p (t i)").bitcast(I32))
         gain_sb = load_by_slice(gain, "gain_sb")
-        nc.sync.dma_start(idx2[:], offs2)
-        load_wgs(0, 1, *HALVES[0])
-        load_page(0)
-        load_wgs(0, 1, *HALVES[1])
-        nc.sync.dma_start(idx3[:], offs3)
         steep_sb = load_by_slice(steep, "steep_sb")
         lift_sb = load_by_slice(lift, "lift_sb")
+        nc.sync.dma_start(idx2[:], offs2)
+        load_wgs(0, 2)
+        load_page(0)
+        load_wgs(2, 2)
+        nc.sync.dma_start(idx3[:], offs3)
         w1_raw[0, 1] = load_rows(w1, 0, BANK, held, "w1_w2_out2")
-        w1_raw[1, 1] = load_rows(w1, 1, BANK, held, "w1_scratch")
-        load_wgs(1, 2, 0, S)
         load_page(1)
-        load_wgs(2, 4, 0, S)
+        w1_raw[1, 1] = load_rows(w1, 1, BANK, held, "w1_scratch")
+        load_wgs(4, 4)
         load_page(2)
 
         w1_q = {}
@@ -267,8 +265,7 @@ def tile_list_seaweed_harvest_page_kernel(
         for first, count in QUARTERS[2:]:
             make_factors(0, first, count)
         multiply(0, QUARTERS[2:], table.tile([P, BANK], F32, name="weighted0", offset=20 * KIB))
-        for first, count in QUARTERS[2:]:
-            put(0, first, count)
+        put(0, *HALVES[1])
         for first, count in HALVES:
             make_factors(1, first, count)
         new_h(1)

import math
from contextlib import ExitStack

import concourse.mybir as mybir

K, T, S, H, N, M, T2 = 1024, 4096, 1024, 1024, 512, 1024, 2048
FLOPS = 2 * K * H * S + 4 * H * N * M

F32 = mybir.dt.float32
BF16 = mybir.dt.bfloat16
I32 = mybir.dt.int32
U32 = mybir.dt.uint32
U16 = mybir.dt.uint16
U8 = mybir.dt.uint8
FP8X4 = mybir.dt.float8_e4m3fn_x4
FP4X4 = mybir.dt.float4_e2m1fn_x4
ACT = mybir.ActivationFunctionType
MULT = mybir.AluOpType.mult
ADD = mybir.AluOpType.add

P = 128
BANK = 512
KIB = 1024
SLICES = 8
PAGE_SLOTS = 3
HALVES = [(0, BANK), (BANK, BANK)]
QUARTERS = [(first, BANK // 2) for first in range(0, S, BANK // 2)]
RUNS = [HALVES, [QUARTERS[0], QUARTERS[1], HALVES[1]]]


def tile_list_seaweed_harvest_page_kernel(
    tc, tab_words, tab_scales, offs, w1, gain, page0, offs2, wgs, offs3, steep, lift, w2, w3_words, w3_scales,
    page1, offs4, wgo, out,
):
    nc = tc.nc
    with ExitStack() as ctx:
        held = ctx.enter_context(tc.tile_pool(name="held", bufs=1))
        raws = ctx.enter_context(tc.tile_pool(name="raws", bufs=2))
        pages = ctx.enter_context(tc.tile_pool(name="pages", bufs=1))
        work = ctx.enter_context(tc.tile_pool(name="work", bufs=4))
        table = ctx.enter_context(tc.tile_pool(name="table", bufs=1))
        psum = ctx.enter_context(tc.psum_pool(name="psum", bufs=8))

        idx, idx2, idx3, idx4 = [held.tile([P, S // 16], U16, name="list%d" % i) for i in range(4)]

        def entries(tile, first, count):
            return tile[:, first // 16 : (first + count) // 16]

        def load_rows(w, a, first_col, pool, tag):
            raw = pool.tile([P, 4, BANK], F32, name="raw", tag=tag)
            rows = w[BANK * a : BANK * (a + 1), first_col : first_col + BANK]
            nc.sync.dma_start(raw[:], rows.rearrange("(p j) c -> p j c", j=4))
            return raw

        def page_slot(shape, name, s):
            return pages.tile(shape, F32, name=name, offset=4 * T2 * (s % PAGE_SLOTS))

        page_sb = {}

        def load_page(s):
            page_sb[s] = page_slot([P, T2], "page%d" % s, s)
            nc.sync.dma_start(page_sb[s][:], page0.rearrange("(b p t) c -> b t p c", b=2, t=4)[s // 4, s % 4])

        wgs_sb = {}

        def load_wgs(first_half, halves):
            tile = held.tile([P, halves, BANK], F32, name="wgs%d" % first_half)
            source = wgs.rearrange("(q t) (h j) -> q (t h) j", t=4, h=2)[:, first_half : first_half + halves, :]
            for quad in (0, 2, 1, 3):
                nc.sync.dma_start(tile[32 * quad : 32 * quad + 32], source)
            for i in range(halves):
                wgs_sb[divmod(first_half + i, 2)] = tile[:, i, :]

        def load_by_slice(vec, name):
            tile = held.tile([P, 2, 4], F32, name=name)
            nc.sync.dma_start(tile[:], vec.rearrange("(b p t) -> p b t", b=2, t=4))
            return tile

        def new_grouped(width, tag):
            if tag:
                return held.tile([P, 4 * width], BF16, name="grouped", tag=tag, align_bytes=64)
            if width == BANK:
                return work.tile([P, 4 * width], BF16, name="grouped", tag="grouped", bufs=5, align_bytes=64)
            return work.tile([P, 4 * width], BF16, name="quarter", tag="quarter", bufs=3, align_bytes=64)

        def interleave(src, tag=""):
            grouped = new_grouped(src.shape[2], tag)
            nc.scalar.copy(
                grouped[:].rearrange("p (c i j) -> p c j i", i=4, j=4), src.rearrange("p j (c i) -> p c j i", i=4)
            )
            return grouped

        def interleave_dealt(raw, tag):
            grouped = new_grouped(BANK, tag)
            nc.scalar.copy(
                grouped[:].rearrange("p (t m j) -> p m t j", t=4, j=4), raw[:].rearrange("p j (m t) -> p m t j", t=4)
            )
            return grouped

        def new_plane(width, name):
            return held.tile([P, width], U8, name=name, align_bytes=64)[:]

        def quantize(grouped, plane, name):
            codes = held.tile([P, plane.shape[1]], U32, name=name, align_bytes=64)
            nc.vector.quantize_mx(out=codes[:].bitcast(FP8X4), scales=plane, in_=grouped[:])
            return codes, plane

        zero_in = held.tile([P, 1], F32, name="zero_in")
        zero = held.tile([P, 1], F32, name="zero")
        nc.vector.memset(zero_in[:], 0.0)
        nc.scalar.activation(zero[:], zero_in[:], ACT.Silu)

        tab_plane = table.tile([P, T], U8, name="tab_plane", align_bytes=64, offset=33 * KIB)
        nc.vector.memset(tab_plane[:].bitcast(I32), 0)
        for quad in range(4):
            nc.gpsimd.dma_start(
                tab_plane[32 * quad : 32 * quad + 8, :].bitcast(I32),
                tab_scales[:, 4 * quad : 4 * quad + 4, :].bitcast(I32),
            )
        w3_plane = held.tile([P, 2, N], U8, name="w3_plane", align_bytes=64)
        nc.vector.memset(w3_plane[:].rearrange("p a n -> p (a n)").bitcast(I32), 0)

        nc.sync.dma_start(idx[:], offs)
        w1_raw = {(a, 0): load_rows(w1, a, 0, raws, "raw") for a in range(2)}
        tab_sb = []
        for a, offset in enumerate((17 * KIB, 0)):
            tab_sb.append(table.tile([P, T], I32, name="tab%d" % a, align_bytes=64, offset=offset))
            nc.sync.dma_start(tab_sb[a][:], tab_words[a].rearrange("p t i -> p (t i)").bitcast(I32))
        gain_sb = load_by_slice(gain, "gain_sb")
        steep_sb = load_by_slice(steep, "steep_sb")
        lift_sb = load_by_slice(lift, "lift_sb")
        nc.sync.dma_start(idx2[:], offs2)
        load_wgs(0, 2)
        load_page(0)
        load_wgs(2, 2)
        nc.sync.dma_start(idx3[:], offs3)
        w1_raw[0, 1] = load_rows(w1, 0, BANK, held, "w1_w2_out2")
        load_page(1)
        w1_raw[1, 1] = load_rows(w1, 1, BANK, held, "w1_scratch")
        load_wgs(4, 4)
        load_page(2)

        w1_q = {}
        for a, tag in enumerate(("", "w1_words")):
            w1_q[a, 0] = quantize(interleave_dealt(w1_raw[a, 0], tag), new_plane(BANK, "w1s%d0" % a), "w1q%d0" % a)
        v0 = held.tile([P, S], U32, name="v0", tag="w1_words", align_bytes=64)
        nc.vector.tensor_copy(v0[:], tab_sb[0][:].bitcast(U32).indirect(idx[:]))
        v_plane = table.tile([P, S], U8, name="v_plane", align_bytes=64, offset=32 * KIB)
        nc.vector.tensor_copy(v_plane[:], tab_plane[:].indirect(idx[:]))
        v_words = {}
        for half, (first, count) in enumerate(HALVES):
            v1 = table.tile([P, count], U32, name="v1_%d" % half, align_bytes=64, offset=33 * KIB + 4 * first)
            nc.vector.tensor_copy(v1[:], tab_sb[1][:].bitcast(U32).indirect(entries(idx, first, count)))
            v_words[0, half], v_words[1, half] = v0[:, first : first + count], v1[:]

        half_steep = held.tile([P, 2, 4], F32, name="half_steep")
        neg_half_lift = held.tile([P, 2, 4], F32, name="neg_half_lift")
        nc.gpsimd.tensor_scalar(half_steep[:], steep_sb[:], 0.5, 0.0, MULT, ADD)
        nc.gpsimd.tensor_scalar(neg_half_lift[:], lift_sb[:], -0.5, 0.0, MULT, ADD)

        scratch = [held.tile([P, 2, BANK], F32, name="scratch", tag="scratch_w2_out3")]
        scratch_uses = []

        def next_scratch(count):
            scratch_uses.append(count)
            return scratch[-1][:, len(scratch_uses) % 2, 0:count]

        def product(s, first, count):
            b, t = divmod(s, 4)
            half, inner = divmod(first, BANK)
            bank = psum.tile([P, BANK], F32, name="bank", tag="bank")[:, 0:count]
            for a in range(2):
                codes, plane = w1_q[a, b]
                nc.tensor.matmul_mx(
                    out=bank,
                    lhsT=codes[:, t * P : (t + 1) * P].bitcast(FP8X4),
                    lhsT_scale=plane[:, t * P : (t + 1) * P],
                    rhs=v_words[a, half][:, inner : inner + count].bitcast(FP8X4),
                    rhs_scale=v_plane[4 * a : P, first : first + count],
                    start=(a == 0),
                    stop=(a == 1),
                )
            return bank

        def ring(tag, count):
            return work.tile([P, BANK], F32, name=tag, tag=tag)[:, 0:count]

        def weight_buffer(i):
            return held.tile([P, BANK], F32, name="before_weights", tag="weights%d" % i, align_bytes=64)[:]

        def cosine(cos, size):
            nc.scalar.activation(cos, size, ACT.Sin, scale=-1.0, bias=math.pi / 2)

        def gain_of(s):
            return gain_sb[:, s // 4, s % 4 : s % 4 + 1]

        def wgs_of(s, first, count):
            half, inner = divmod(first, BANK)
            return wgs_sb[s % 4, half][:, inner : inner + count]

        factors = {}

        def make_factors(s, first, count):
            bank = product(s, first, count)
            size = weight_buffer(first // BANK) if s == 1 else next_scratch(count)
            cos = weight_buffer(s - 3) if s in (3, 4) and first == 0 else ring("cos", count)
            gained = ring("gained", count)
            nc.scalar.activation(size, bank, ACT.Abs, bias=zero[:])
            nc.scalar.activation(gained, bank, ACT.Copy, scale=gain_of(s))
            cosine(cos, size)
            factors[s, first] = gained, cos

        h_sb = {}

        def new_h(s):
            h_sb[s] = held.tile([P, S], F32, name="h%d" % s, tag="h%d" % (s % 2), align_bytes=64)

        def multiply(s, runs, weighted):
            base = runs[0][0]
            for first, count in runs:
                part = weighted[:, first - base : first - base + count]
                nc.gpsimd.tensor_tensor(part, factors[s, first][1], wgs_of(s, first, count), MULT)
            for first, count in runs:
                part = weighted[:, first - base : first - base + count]
                nc.gpsimd.tensor_tensor(h_sb[s][:, first : first + count], factors[s, first][0], part, MULT)

        def put(s, first, count):
            nc.vector.tensor_copy(
                page_sb[s][:].indirect(entries(idx2, first, count)), h_sb[s][:, first : first + count]
            )

        x_sb, f_sb = {}, {}

        def recall(s):
            b, t = divmod(s, 4)
            if t == 0:
                x_sb[b] = table.tile([P, 4, M], F32, name="x%d" % b, align_bytes=64, offset=16 * KIB * b)
                for first, count in RUNS[b]:
                    f_sb[b, first] = held.tile(
                        [P, 4, count], BF16, name="f%d_%d" % (b, first), tag="f%d" % first, align_bytes=64
                    )
            for first, count in RUNS[b] if s == SLICES - 1 else [(0, M)]:
                nc.vector.tensor_copy(
                    x_sb[b][:, t, first : first + count], page_sb[s][:].indirect(entries(idx3, first, count))
                )

        def squash(s, first, count):
            b, t = divmod(s, 4)
            tanh = next_scratch(count)
            nc.scalar.activation(
                tanh, x_sb[b][:, t, first : first + count], ACT.Tanh, scale=half_steep[:, b, t : t + 1], bias=zero[:]
            )
            factor = neg_half_lift[:, b, t : t + 1]
            nc.scalar.activation(f_sb[b, first][:, t, :], tanh, ACT.Identity, scale=factor, bias=factor)

        new_h(0)
        for first, count in QUARTERS[:2]:
            bank = product(0, first, count)
            size, cos, unweighted = next_scratch(count), ring("cos", count), ring("gained", count)
            nc.scalar.activation(size, bank, ACT.Abs, bias=zero[:])
            cosine(cos, size)
            nc.vector.scalar_tensor_tensor(unweighted, bank, gain_of(0), cos, MULT, MULT)
            nc.vector.tensor_tensor(h_sb[0][:, first : first + count], unweighted, wgs_of(0, first, count), MULT)
            put(0, first, count)
        for first, count in QUARTERS[2:]:
            make_factors(0, first, count)
        multiply(0, QUARTERS[2:], table.tile([P, BANK], F32, name="weighted0", offset=20 * KIB))
        put(0, *HALVES[1])
        for first, count in HALVES:
            make_factors(1, first, count)
        new_h(1)
        multiply(1, HALVES, table.tile([P, S], F32, name="weighted1", offset=24 * KIB))
        for a in range(2):
            grouped = interleave_dealt(w1_raw[a, 1], "weights%d" % a)
            w1_q[a, 1] = quantize(grouped, new_plane(BANK, "w1s%d1" % a), "w1q%d1" % a)
        scratch.append(held.tile([P, 2, BANK], F32, name="scratch", tag="w1_scratch"))
        for first, count in HALVES:
            make_factors(2, first, count)

        w2_tags = ("w1_w2_out2", "scratch_w2_out3")
        w2_grouped, f_grouped, x_grouped, out_sb = {}, {}, {}, {}
        w3_sb = held.tile([P, 2, 2 * N], U8, name="w3_sb", align_bytes=64)
        wgo_sb = held.tile([P, M], F32, name="wgo_sb")

        for s in range(SLICES):
            b, t = divmod(s, 4)
            if s > 0:
                put(s, 0, S)
            recall(s)
            if s + 2 < SLICES:
                new_h(s + 2)
                multiply(s + 2, HALVES, page_slot([P, S], "weighted%d" % (s + 2), s))
            if s + PAGE_SLOTS < SLICES:
                load_page(s + PAGE_SLOTS)
            if s < SLICES - 1:
                for first, count in RUNS[b]:
                    squash(s, first, count)
            if s + 3 < SLICES:
                for first, count in HALVES:
                    make_factors(s + 3, first, count)
            if s in (1, 2):
                w2_raw = load_rows(w2, s - 1, 0, held, w2_tags[s - 1])
                w2_grouped[s - 1] = interleave(w2_raw[:], "weights%d" % (s - 1))
            if s == 3:
                for first, count in HALVES:
                    f_grouped[first] = interleave(f_sb[0, first][:])
            if s in (4, 5):
                first, count = HALVES[s - 4]
                x_grouped[first] = interleave(x_sb[0][:, :, first : first + count])
            if s == 2:
                nc.sync.dma_start(w3_sb[:].bitcast(I32), w3_words.rearrange("a p c -> p a c").bitcast(I32))
                for quad in range(4):
                    nc.sync.dma_start(
                        w3_plane[32 * quad : 32 * quad + 4].bitcast(I32),
                        w3_scales[:, 4 * quad : 4 * quad + 4, :].rearrange("a r n -> r a n").bitcast(I32),
                    )
                nc.sync.dma_start(idx4[:], offs4)
                nc.sync.dma_start(wgo_sb[:], wgo)
            if b == 1:
                pool, tag = (raws, "raw") if t < 2 else (held, w2_tags[t - 2])
                out_sb[t] = pool.tile([P, T2], F32, name="harvest", tag=tag)
                nc.sync.dma_start(out_sb[t][:], page1[t * P : (t + 1) * P, :])

        early = held.tile([P, 4, BANK], U8, name="early_planes", tag="h%d" % ((SLICES - 1) % 2), align_bytes=64)
        w2_q = [quantize(w2_grouped[a], early[:, a, :], "w2q%d" % a) for a in range(2)]
        x_q = {(0, 0): quantize(x_grouped[0], early[:, 2, :], "xq0_0")}
        f_q = {(0, 0): quantize(f_grouped[0], early[:, 3, :], "fq0_0")}

        def finish_f(first, count):
            squash(SLICES - 1, first, count)
            grouped = interleave(f_sb[1, first][:])
            f_q[1, first] = quantize(grouped, new_plane(count, "fs1_%d" % first), "fq1_%d" % first)

        def finish_x(first, count):
            grouped = interleave(x_sb[1][:, :, first : first + count])
            x_q[1, first] = quantize(grouped, new_plane(count, "xs1_%d" % first), "xq1_%d" % first)

        def harvest(n, first, count):
            bank = psum.tile([P, BANK], F32, name="bank", tag="bank")
            rows = slice(n * P, (n + 1) * P)
            passes = []
            for b in (0, 1) if (n, first) == (0, 0) else (1, 0):
                w2_b = w2_q[b][0][:, rows].bitcast(FP8X4), w2_q[b][1][:, rows]
                w3_b = w3_sb[:, b, 2 * n * P : 2 * (n + 1) * P].bitcast(FP4X4), w3_plane[:, b, rows]
                for start, size in RUNS[b]:
                    low, high = max(first, start), min(first + count, start + size)
                    if low < high:
                        width = BANK if high - low == BANK else P
                        passes.append((w2_b, x_q[b, start], low - start, low - first, high - low))
                        for c0 in range(low, high, width):
                            passes.append((w3_b, f_q[b, start], c0 - start, c0 - first, width))
            for i, (weight, (codes, plane), src, dst, width) in enumerate(passes):
                nc.tensor.matmul_mx(
                    out=bank[:, dst : dst + width],
                    lhsT=weight[0],
                    lhsT_scale=weight[1],
                    rhs=codes[:, src : src + width].bitcast(FP8X4),
                    rhs_scale=plane[:, src : src + width],
                    start=(i == 0),
                    stop=(i == len(passes) - 1),
                )
            y = ring("cos", count)
            nc.scalar.copy(y, bank[:, 0:count])
            nc.vector.tensor_tensor(
                out_sb[n][:].indirect(entries(idx4, first, count)), y, wgo_sb[:, first : first + count], MULT
            )
            if first + count == M:
                nc.sync.dma_start(out[rows, :], out_sb[n][:])

        run0, run1, run2 = RUNS[1]
        finish_f(*run0)
        finish_x(*run0)
        late = held.tile([P, 2, BANK], U8, name="late_planes", tag="f0", align_bytes=64)
        x_q[0, BANK] = quantize(x_grouped[BANK], late[:, 0, :], "xq0_1")
        f_q[0, BANK] = quantize(f_grouped[BANK], late[:, 1, :], "fq0_1")
        harvest(0, *run0)
        finish_f(*run1)
        finish_x(*run1)
        harvest(1, *run0)
        harvest(2, *run0)
        harvest(0, *run1)
        finish_f(*run2)
        harvest(1, *run1)
        harvest(2, *run1)
        finish_x(*run2)
        harvest(3, *HALVES[0])
        for n in range(N // P):
            harvest(n, *run2)
